import numpy as np
import ml_dtypes


def mxq(x, axis, fmt="e4m3"):
    dtype, down = {"e4m3": (ml_dtypes.float8_e4m3fn, 7), "e5m2": (ml_dtypes.float8_e5m2, 14)}[fmt]
    v = np.moveaxis(np.asarray(x, np.float32).astype(ml_dtypes.bfloat16).astype(np.float64), axis, -1)
    blocks = v.reshape(v.shape[:-1] + (-1, 32))
    amax = np.abs(blocks).max(-1, keepdims=True)
    byte = np.maximum(np.where(amax > 0, np.frexp(amax)[1] - 1 + 127, 0) - down, 1)
    scale = np.exp2(byte - 127.0)
    codes = (blocks / scale).astype(np.float32).astype(dtype).astype(np.float64)
    return np.moveaxis((codes * scale).reshape(v.shape), -1, axis)


WIDE = False


def mx_kscale(k):
    if not WIDE:
        return np.ones(k)
    levels = np.array([10, -10, 5, -5, 0])
    if k % 512:
        return np.exp2(np.random.permutation(np.resize(levels, k // 32))).repeat(32)
    a = np.empty((k // 512, 16))
    for p in range(k // 512):
        a[p, :8] = np.random.permutation(np.resize(levels, 8))
        for g in range(8):
            far = levels[np.abs(levels - a[p, g]) >= 10]
            a[p, g + 8] = far[np.random.randint(len(far))]
    return np.exp2(a.ravel()).repeat(32)


def f64(x):
    return np.asarray(x).astype(np.float64)


def striped(idx):
    return np.tile(idx.reshape(-1, 16).T, (8, 1)).astype(np.uint16)


def unstriped(offs):
    return offs[:16].T.reshape(-1).astype(np.int64)


def pack_weight(w):
    k, n = w.shape
    w = f64(np.asarray(w, np.float32).astype(ml_dtypes.bfloat16)).reshape(k // 32, 32, n)
    amax = np.abs(w).max(1)
    byte = np.clip(np.where(amax > 0, np.frexp(amax)[1] - 1 + 127 - 7, 1), 1, 254)
    scaled = (w * np.exp2(127.0 - byte)[:, None, :]).reshape(k, n).astype(np.float32)
    words = np.ascontiguousarray(scaled.reshape(k // 512, 128, 4, n).transpose(0, 1, 3, 2)).astype(ml_dtypes.float8_e4m3fn).view(np.uint8)
    return words, np.ascontiguousarray(byte.astype(np.uint8).reshape(k // 512, 16, n))


def unpack_weight(words, scales):
    g, p, n, _ = words.shape
    vals = np.ascontiguousarray(words).view(ml_dtypes.float8_e4m3fn).astype(np.float64) * np.repeat(np.exp2(scales.astype(np.float64) - 127.0), 8, axis=1)[..., None]
    return vals.transpose(0, 1, 3, 2).reshape(g * 512, n)


E2M1 = np.array([0.0, 0.5, 1.0, 1.5, 2.0, 3.0, 4.0, 6.0, -0.0, -0.5, -1.0, -1.5, -2.0, -3.0, -4.0, -6.0])


def pack_fp4(w):
    k, n = w.shape
    w = f64(np.asarray(w, np.float32).astype(ml_dtypes.bfloat16)).reshape(k // 32, 32, n)
    amax = np.abs(w).max(1)
    mant, ex = np.frexp(amax / 6.0)
    byte = np.clip(np.where(amax > 0, np.where(mant > 0.5, ex, ex - 1) + 127, 1), 1, 254)
    scaled = (w * np.exp2(127.0 - byte)[:, None, :]).reshape(k, n).astype(np.float32)
    c = np.ascontiguousarray(scaled.reshape(k // 512, 128, 4, n).transpose(0, 1, 3, 2)).astype(ml_dtypes.float4_e2m1fn).view(np.uint8) & 0xF
    words = (c[..., 0::2] | (c[..., 1::2] << 4)).reshape(k // 512, 128, 2 * n)
    return np.ascontiguousarray(words), np.ascontiguousarray(byte.astype(np.uint8).reshape(k // 512, 16, n))


def unpack_fp4(words, scales):
    g, _, n = scales.shape
    words = np.ascontiguousarray(words).reshape(g, 128, n, 2)
    nib = np.empty((g, 128, n, 4), np.uint8)
    nib[..., 0::2] = words & 0xF
    nib[..., 1::2] = words >> 4
    vals = E2M1[nib] * np.repeat(np.exp2(scales.astype(np.float64) - 127.0), 8, axis=1)[..., None]
    return vals.transpose(0, 1, 3, 2).reshape(g * 512, n)


def sigmoid(v):
    return 1.0 / (1.0 + np.exp(-np.maximum(v, -700.0)))


K, T, S, N, H = 512, 2048, 512, 256, 512


def setup_inputs():
    n = np.random.standard_normal
    s = mx_kscale(K)[:, None]
    u = mx_kscale(H)
    packed_xT = pack_weight(n((K, T)) * s)
    packed_w1 = pack_fp4(n((K, H)) / np.sqrt(K) / s)
    packed_w2 = pack_fp4(n((K, H)) / np.sqrt(K) / s)
    packed_w3 = pack_fp4(n((H, N)) / np.sqrt(H) / u[:, None])
    return {
        "x_words": packed_xT[0],
        "x_scales": packed_xT[1],
        "w1_words": packed_w1[0],
        "w1_scales": packed_w1[1],
        "w2_words": packed_w2[0],
        "w2_scales": packed_w2[1],
        "rup": (np.random.uniform(0.2, 0.6, (H, S))).astype(np.float32),
        "rdn": (np.random.uniform(0.2, 0.6, (H, S))).astype(np.float32),
        "unit": (np.random.uniform(0.6, 1.4, (H, 1)) * u[:, None]).astype(np.float32),
        "w3_words": packed_w3[0],
        "w3_scales": packed_w3[1],
        "offs": striped(np.random.permutation(T)[:S]),
        "prv": striped(np.random.permutation(S)),
    }


def reference(x_words, x_scales, w1_words, w1_scales, w2_words, w2_scales, rup, rdn, unit, w3_words, w3_scales, offs, prv):
    xq = unpack_weight(x_words, x_scales)[:, unstriped(offs)]
    us = unpack_fp4(w2_words, w2_scales).T @ xq
    on = sigmoid(2.0 * us)
    y = unpack_fp4(w1_words, w1_scales).T @ xq
    pow_ = on * (0.6 * (np.log(np.exp(y) + 1.0)) + 0.3)
    pp = pow_[:, unstriped(prv)]
    ramp = np.maximum(np.minimum(pow_ - pp, f64(rup)), -1.0 * f64(rdn))
    hid = f64(unit) * ((pow_[:, unstriped(prv)] + ramp) * on)
    return unpack_fp4(w3_words, w3_scales).T @ mxq(hid, 0, "e4m3")

@@ -1,0 +1,222 @@
+from contextlib import ExitStack
+
+import concourse.mybir as mybir
+
+K, T, S, N, H = 512, 2048, 512, 256, 512
+FLOPS = 2 * (2 * K * H * S + H * N * S)
+
+P = 128
+PACK = 4
+QUADS = 4
+F32 = mybir.dt.float32
+BF16 = mybir.dt.bfloat16
+I32 = mybir.dt.int32
+U32 = mybir.dt.uint32
+U16 = mybir.dt.uint16
+U8 = mybir.dt.uint8
+FP8X4 = mybir.dt.float8_e4m3fn_x4
+FP4X4 = mybir.dt.float4_e2m1fn_x4
+ALU = mybir.AluOpType
+ACT = mybir.ActivationFunctionType
+
+TINY = 2.0 ** -60
+PIECES = ((0, 256), (256, 512))
+
+
+def load_scale_rows(queue, plane, scales, quads=range(QUADS)):
+    for q in quads:
+        queue.dma_start(
+            out=plane[32 * q : 32 * q + 4, :].bitcast(I32),
+            in_=scales[0, 4 * q : 4 * q + 4, :].bitcast(I32),
+        )
+
+
+def tile_picked_yunitc_ramp_p_kernel(
+    tc, x_words, x_scales, w1_words, w1_scales, w2_words, w2_scales, rup, rdn, unit, w3_words, w3_scales, offs, prv, out
+):
+    nc = tc.nc
+    with ExitStack() as ctx:
+        lists = ctx.enter_context(tc.tile_pool(name="lists", bufs=1))
+        keep = ctx.enter_context(tc.tile_pool(name="keep", bufs=1))
+        psum = ctx.enter_context(tc.psum_pool(name="psum", bufs=1))
+
+        offs_t = lists.tile([P, S // 16], U16, name="offs_t")
+        prv_t = lists.tile([P, S // 16], U16, name="prv_t")
+
+        x_plane = keep.tile([P, T], U8, name="x_plane", align_bytes=64)
+        w1_plane = keep.tile([P, H], U8, name="w1_plane", align_bytes=64)
+        w2_plane = keep.tile([P, H], U8, name="w2_plane", align_bytes=64)
+        w3_plane = keep.tile([P, N], U8, name="w3_plane", align_bytes=64)
+        nc.gpsimd.memset(w1_plane[:].bitcast(I32), 0)
+        nc.gpsimd.memset(x_plane[:].bitcast(I32), 0)
+        nc.gpsimd.memset(w2_plane[:].bitcast(I32), 0)
+        nc.gpsimd.memset(w3_plane[:].bitcast(I32), 0)
+
+        x_table = keep.tile([P, T], U32, name="x_table", align_bytes=64)
+        w1_raw = keep.tile([P, 2 * H], U8, name="w1_raw", align_bytes=64)
+        w2_raw = keep.tile([P, 2 * H], U8, name="w2_raw", align_bytes=64)
+        w3_codes = keep.tile([P, 2 * N], U8, name="w3_codes", align_bytes=64)
+        unit_t = keep.tile([P, PACK], F32, name="unit_t")
+
+        nc.sync.dma_start(offs_t[:], offs)
+        nc.sync.dma_start(out=w1_raw[:].bitcast(I32), in_=w1_words[0].bitcast(I32))
+        nc.sync.dma_start(out=w2_raw[:].bitcast(I32), in_=w2_words[0].bitcast(I32))
+        load_scale_rows(nc.sync, w1_plane, w1_scales, range(1))
+        nc.sync.dma_start(out=x_table[:].bitcast(I32), in_=x_words[0].rearrange("p c r -> p (c r)").bitcast(I32))
+        load_scale_rows(nc.sync, x_plane, x_scales)
+        load_scale_rows(nc.sync, w1_plane, w1_scales, range(1, QUADS))
+        load_scale_rows(nc.sync, w2_plane, w2_scales)
+        rup_v = rup.rearrange("(p t) j -> p t j", t=PACK)
+        rdn_v = rdn.rearrange("(p t) j -> p t j", t=PACK)
+        rdn_t, rup_t = [], []
+        for h in range(2):
+            dn = keep.tile([P, 2, S], F32, name="rdn%d" % h)
+            up = keep.tile([P, 2, S], F32, name="rup%d" % h)
+            nc.sync.dma_start(out=dn[:], in_=rdn_v[:, 2 * h : 2 * h + 2, :])
+            nc.sync.dma_start(out=up[:], in_=rup_v[:, 2 * h : 2 * h + 2, :])
+            rdn_t.append(dn)
+            rup_t.append(up)
+        nc.sync.dma_start(prv_t[:], prv)
+        nc.sync.dma_start(out=unit_t[:], in_=unit.rearrange("(p t) o -> p (t o)", t=PACK))
+        nc.sync.dma_start(out=w3_codes[:].bitcast(I32), in_=w3_words[0].bitcast(I32))
+        load_scale_rows(nc.sync, w3_plane, w3_scales)
+
+        w1_codes = keep.tile([P, 2 * H], U8, name="w1_codes", align_bytes=64)
+        w2_codes = keep.tile([P, 2 * H], U8, name="w2_codes", align_bytes=64)
+        w1_dealt = keep.tile([P, H], U8, name="w1_dealt", align_bytes=64)
+        w2_dealt = keep.tile([P, H], U8, name="w2_dealt", align_bytes=64)
+        x_codes = keep.tile([P, S], U32, name="x_codes", align_bytes=64)
+        x_picked = keep.tile([P, S], U8, name="x_picked", align_bytes=64)
+
+        def deal_words(dst, src):
+            nc.vector.tensor_copy(
+                out=dst[:].rearrange("p (t m b) -> p t m b", t=PACK, b=2),
+                in_=src[:].rearrange("p (m t b) -> p t m b", t=PACK, b=2),
+            )
+
+        def deal_bytes(dst, src):
+            nc.vector.tensor_copy(
+                out=dst[:].rearrange("p (t m) -> p t m", t=PACK),
+                in_=src[:].rearrange("p (m t) -> p t m", t=PACK),
+            )
+
+        deal_words(w1_codes, w1_raw)
+        nc.vector.tensor_copy(x_picked[:], x_plane[:].indirect(offs_t[:]))
+        deal_bytes(w1_dealt, w1_plane)
+        nc.vector.tensor_copy(x_codes[:], x_table[:].indirect(offs_t[:]))
+        deal_words(w2_codes, w2_raw)
+        deal_bytes(w2_dealt, w2_plane)
+
+        def first_product(tag, codes, plane, t):
+            bank = psum.tile([P, S], F32, name=tag, tag=tag)
+            nc.tensor.matmul_mx(
+                out=bank[:],
+                lhsT=codes[:, 2 * P * t : 2 * P * (t + 1)].bitcast(FP4X4),
+                lhsT_scale=plane[:, P * t : P * (t + 1)],
+                rhs=x_codes[:].bitcast(FP8X4),
+                rhs_scale=x_picked[:],
+                start=True,
+                stop=True,
+            )
+            return bank
+
+        y = [first_product("bank%d" % t, w1_codes, w1_dealt, t) for t in range(PACK)]
+        us = [first_product("bank%d" % (PACK + t), w2_codes, w2_dealt, t) for t in range(PACK)]
+
+        window = [keep.tile([P, 2 * S], F32, name="window%d" % t) for t in range(PACK)]
+        sig = [keep.tile([P, S], F32, name="sig%d" % t) for t in range(PACK)]
+        lns = [keep.tile([P, S], F32, name="lns%d" % t) for t in range(PACK)]
+        nsp = [keep.tile([P, S], F32, name="nsp%d" % t) for t in range(PACK)]
+        pp = [keep.tile([P, S], F32, name="pp%d" % t) for t in range(PACK)]
+        low = [keep.tile([P, S], F32, name="low%d" % t) for t in range(PACK)]
+        over = [keep.tile([P, S], F32, name="over%d" % t) for t in range(PACK)]
+        cut = [keep.tile([P, S], F32, name="cut%d" % t) for t in range(PACK)]
+        held = [keep.tile([P, S], F32, name="held%d" % t) for t in range(PACK)]
+        span = [keep.tile([P, 2, S], F32, name="span%d" % h) for h in range(2)]
+        hid = [keep.tile([P, PACK, b - a], BF16, name="hid%d" % i) for i, (a, b) in enumerate(PIECES)]
+
+        for t in range(PACK):
+            nc.scalar.activation(sig[t][:], y[t][:], ACT.Sigmoid, scale=-1.0)
+        for t in range(PACK):
+            nc.scalar.activation(window[t][:, S:], us[t][:], ACT.Sigmoid, scale=2.0)
+        for h in range(2):
+            nc.vector.tensor_tensor(span[h][:], rup_t[h][:], rdn_t[h][:], ALU.add)
+        for t in range(PACK):
+            nc.scalar.activation(lns[t][:], sig[t][:], ACT.Ln, bias=TINY)
+
+        def softplus(t):
+            nc.vector.scalar_tensor_tensor(nsp[t][:], y[t][:], -1.0, lns[t][:], ALU.mult, ALU.min)
+
+        def power(t):
+            nc.vector.scalar_tensor_tensor(window[t][:, :S], nsp[t][:], -0.5, window[t][:, S:], ALU.add, ALU.mult)
+            nc.scalar.activation(pp[t][:], window[t][:].indirect(prv_t[:]), ACT.Copy, scale=-0.6)
+
+        softplus(0)
+        for t in range(PACK):
+            if t + 1 < PACK:
+                softplus(t + 1)
+            power(t)
+
+        def ramp_steps(t, a, b):
+            h, u = divmod(t, 2)
+            dn = rdn_t[h][:, u, a:b]
+            steps = [
+                lambda: nc.vector.tensor_tensor(low[t][:, a:b], pp[t][:, a:b], dn, ALU.subtract),
+                lambda: nc.vector.scalar_tensor_tensor(
+                    over[t][:, a:b], window[t][:, a:b], -0.6, low[t][:, a:b], ALU.mult, ALU.subtract
+                ),
+                lambda: nc.vector.tensor_tensor(cut[t][:, a:b], over[t][:, a:b], span[h][:, u, a:b], ALU.min),
+                lambda: nc.vector.scalar_tensor_tensor(
+                    held[t][:, a:b], cut[t][:, a:b], 0.0, low[t][:, a:b], ALU.max, ALU.add
+                ),
+            ]
+            return steps
+
+        def hidden(t, i):
+            a, b = PIECES[i]
+            nc.vector.scalar_tensor_tensor(
+                hid[i][:, t, :], held[t][:, a:b], unit_t[:, t : t + 1], window[t][:, S + a : S + b], ALU.mult, ALU.mult
+            )
+
+        out_v = out.rearrange("(a p) j -> p a j", p=P)
+
+        def last_product(i, engine_copy):
+            a, b = PIECES[i]
+            n = b - a
+            woven = keep.tile([P, n, PACK], BF16, name="woven%d" % i, align_bytes=64)
+            codes = keep.tile([P, n], U32, name="hcodes%d" % i, align_bytes=64)
+            plane = keep.tile([P, n], U8, name="hplane%d" % i, align_bytes=64)
+            engine_copy(out=woven[:], in_=hid[i][:].rearrange("p t j -> p j t"))
+            nc.vector.quantize_mx(
+                out=codes[:].bitcast(FP8X4), scales=plane[:], in_=woven[:].rearrange("p j t -> p (j t)")
+            )
+            tag = "bank%d" % (PACK + i)
+            bank = psum.tile([P, S], F32, name="zones%d" % i, tag=tag)
+            for m in range(N // P):
+                nc.tensor.matmul_mx(
+                    out=bank[:, m * n : (m + 1) * n],
+                    lhsT=w3_codes[:, 2 * P * m : 2 * P * (m + 1)].bitcast(FP4X4),
+                    lhsT_scale=w3_plane[:, P * m : P * (m + 1)],
+                    rhs=codes[:].bitcast(FP8X4),
+                    rhs_scale=plane[:],
+                    start=True,
+                    stop=True,
+                )
+            res = keep.tile([P, N // P, n], F32, name="res%d" % i)
+            nc.scalar.copy(out=res[:].rearrange("p a j -> p (a j)"), in_=bank[:, : (N // P) * n])
+            nc.sync.dma_start(out=out_v[:, :, a:b], in_=res[:])
+
+        for s0, s1 in zip(ramp_steps(0, 0, S), ramp_steps(1, 0, S)):
+            s0()
+            s1()
+        for i in range(len(PIECES)):
+            hidden(0, i)
+            hidden(1, i)
+        for i, (a, b) in enumerate(PIECES):
+            for s0, s1 in zip(ramp_steps(2, a, b), ramp_steps(3, a, b)):
+                s0()
+                s1()
+            hidden(2, i)
+            hidden(3, i)
+            last = i == len(PIECES) - 1
+            last_product(i, nc.vector.tensor_copy if last else nc.scalar.copy)

@@ -1,6 +1,7 @@
 from contextlib import ExitStack
 
 import concourse.mybir as mybir
+from concourse.masks import make_identity
 
 K, T, S, N, H = 512, 2048, 512, 256, 512
 FLOPS = 2 * (2 * K * H * S + H * N * S)
@@ -8,6 +9,7 @@ FLOPS = 2 * (2 * K * H * S + H * N * S)
 P = 128
 PACK = 4
 QUADS = 4
+HALF = S // 2
 F32 = mybir.dt.float32
 BF16 = mybir.dt.bfloat16
 I32 = mybir.dt.int32
@@ -20,7 +22,8 @@ ALU = mybir.AluOpType
 ACT = mybir.ActivationFunctionType
 
 TINY = 2.0 ** -60
-PIECES = ((0, 256), (256, 512))
+TURNED = 2
+PIECES = ((0, 256), (256, 384), (384, 512))
 
 
 def load_scale_rows(queue, plane, scales, quads=range(QUADS)):
@@ -40,53 +43,57 @@ def tile_picked_yunitc_ramp_p_kernel(
         keep = ctx.enter_context(tc.tile_pool(name="keep", bufs=1))
         psum = ctx.enter_context(tc.psum_pool(name="psum", bufs=1))
 
+        def sbuf(shape, dtype, name, slot=None):
+            return keep.tile(shape, dtype, name=name, tag=slot or name, align_bytes=64)
+
         offs_t = lists.tile([P, S // 16], U16, name="offs_t")
         prv_t = lists.tile([P, S // 16], U16, name="prv_t")
 
-        x_plane = keep.tile([P, T], U8, name="x_plane", align_bytes=64)
-        w1_plane = keep.tile([P, H], U8, name="w1_plane", align_bytes=64)
-        w2_plane = keep.tile([P, H], U8, name="w2_plane", align_bytes=64)
-        w3_plane = keep.tile([P, N], U8, name="w3_plane", align_bytes=64)
-        nc.gpsimd.memset(w1_plane[:].bitcast(I32), 0)
-        nc.gpsimd.memset(x_plane[:].bitcast(I32), 0)
-        nc.gpsimd.memset(w2_plane[:].bitcast(I32), 0)
-        nc.gpsimd.memset(w3_plane[:].bitcast(I32), 0)
+        x_plane = sbuf([P, T], U8, "x_plane")
+        w1_plane = sbuf([P, H], U8, "w1_plane")
+        w2_plane = sbuf([P, H], U8, "w2_plane")
+        w3_plane = sbuf([P, N], U8, "w3_plane")
+        nc.vector.memset(x_plane[:, : T // 2].bitcast(I32), 0)
+        nc.gpsimd.memset(x_plane[:, T // 2 :].bitcast(I32), 0)
+        for plane in (w1_plane, w2_plane, w3_plane):
+            nc.gpsimd.memset(plane[:].bitcast(I32), 0)
 
-        x_table = keep.tile([P, T], U32, name="x_table", align_bytes=64)
-        w1_raw = keep.tile([P, 2 * H], U8, name="w1_raw", align_bytes=64)
-        w2_raw = keep.tile([P, 2 * H], U8, name="w2_raw", align_bytes=64)
-        w3_codes = keep.tile([P, 2 * N], U8, name="w3_codes", align_bytes=64)
-        unit_t = keep.tile([P, PACK], F32, name="unit_t")
+        x_table = sbuf([P, T], U32, "x_table")
+        w1_raw = sbuf([P, 2 * H], U8, "w1_raw")
+        w2_raw = sbuf([P, 2 * H], U8, "w2_raw")
+        w3_codes = sbuf([P, 2 * N], U8, "w3_codes")
+        unit_t = sbuf([P, PACK], F32, "unit_t")
+        rdn_t = [sbuf([P, 2, S], F32, "rdn%d" % h) for h in range(2)]
+        rup_t = [sbuf([P, 2, S], F32, "rup%d" % h) for h in range(2)]
 
         nc.sync.dma_start(offs_t[:], offs)
-        nc.sync.dma_start(out=w1_raw[:].bitcast(I32), in_=w1_words[0].bitcast(I32))
-        nc.sync.dma_start(out=w2_raw[:].bitcast(I32), in_=w2_words[0].bitcast(I32))
-        load_scale_rows(nc.sync, w1_plane, w1_scales, range(1))
+        nc.scalar.dma_start(out=w1_raw[:].bitcast(I32), in_=w1_words[0].bitcast(I32))
+        load_scale_rows(nc.sync, x_plane, x_scales, (0, 2))
+        load_scale_rows(nc.scalar, x_plane, x_scales, (1, 3))
         nc.sync.dma_start(out=x_table[:].bitcast(I32), in_=x_words[0].rearrange("p c r -> p (c r)").bitcast(I32))
-        load_scale_rows(nc.sync, x_plane, x_scales)
-        load_scale_rows(nc.sync, w1_plane, w1_scales, range(1, QUADS))
-        load_scale_rows(nc.sync, w2_plane, w2_scales)
+        load_scale_rows(nc.scalar, w1_plane, w1_scales)
+        load_scale_rows(nc.sync, w2_plane, w2_scales, (0, 1))
+        nc.sync.dma_start(out=w2_raw[:].bitcast(I32), in_=w2_words[0].bitcast(I32))
+        load_scale_rows(nc.gpsimd, w2_plane, w2_scales, (2, 3))
         rup_v = rup.rearrange("(p t) j -> p t j", t=PACK)
         rdn_v = rdn.rearrange("(p t) j -> p t j", t=PACK)
-        rdn_t, rup_t = [], []
         for h in range(2):
-            dn = keep.tile([P, 2, S], F32, name="rdn%d" % h)
-            up = keep.tile([P, 2, S], F32, name="rup%d" % h)
-            nc.sync.dma_start(out=dn[:], in_=rdn_v[:, 2 * h : 2 * h + 2, :])
-            nc.sync.dma_start(out=up[:], in_=rup_v[:, 2 * h : 2 * h + 2, :])
-            rdn_t.append(dn)
-            rup_t.append(up)
+            nc.sync.dma_start(out=rdn_t[h][:], in_=rdn_v[:, 2 * h : 2 * h + 2, :])
+            nc.sync.dma_start(out=rup_t[h][:], in_=rup_v[:, 2 * h : 2 * h + 2, :])
         nc.sync.dma_start(prv_t[:], prv)
         nc.sync.dma_start(out=unit_t[:], in_=unit.rearrange("(p t) o -> p (t o)", t=PACK))
         nc.sync.dma_start(out=w3_codes[:].bitcast(I32), in_=w3_words[0].bitcast(I32))
         load_scale_rows(nc.sync, w3_plane, w3_scales)
 
-        w1_codes = keep.tile([P, 2 * H], U8, name="w1_codes", align_bytes=64)
-        w2_codes = keep.tile([P, 2 * H], U8, name="w2_codes", align_bytes=64)
-        w1_dealt = keep.tile([P, H], U8, name="w1_dealt", align_bytes=64)
-        w2_dealt = keep.tile([P, H], U8, name="w2_dealt", align_bytes=64)
-        x_codes = keep.tile([P, S], U32, name="x_codes", align_bytes=64)
-        x_picked = keep.tile([P, S], U8, name="x_picked", align_bytes=64)
+        ident = sbuf([P, P], F32, "ident")
+        make_identity(nc, ident[:])
+
+        w1_codes = sbuf([P, 2 * H], U8, "w1_codes")
+        w2_codes = sbuf([P, 2 * H], U8, "w2_codes")
+        w1_high = sbuf([P, H // 2], U8, "w1_high")
+        w2_dealt = sbuf([P, H], U8, "w2_dealt")
+        x_codes = sbuf([P, S], U32, "x_codes")
+        x_picked = sbuf([P, S], U8, "x_picked")
 
         def deal_words(dst, src):
             nc.vector.tensor_copy(
@@ -94,107 +101,174 @@ def tile_picked_yunitc_ramp_p_kernel(
                 in_=src[:].rearrange("p (m t b) -> p t m b", t=PACK, b=2),
             )
 
-        def deal_bytes(dst, src):
+        def deal_bytes(dst, src, t0=0, t1=PACK):
             nc.vector.tensor_copy(
-                out=dst[:].rearrange("p (t m) -> p t m", t=PACK),
-                in_=src[:].rearrange("p (m t) -> p t m", t=PACK),
+                out=dst[:].rearrange("p (t m) -> p t m", m=P),
+                in_=src[:].rearrange("p (m t) -> p t m", t=PACK)[:, t0:t1, :],
             )
 
         deal_words(w1_codes, w1_raw)
         nc.vector.tensor_copy(x_picked[:], x_plane[:].indirect(offs_t[:]))
-        deal_bytes(w1_dealt, w1_plane)
-        nc.vector.tensor_copy(x_codes[:], x_table[:].indirect(offs_t[:]))
+        deal_bytes(w1_high, w1_plane, 2, 4)
+        for c in range(2):
+            nc.vector.tensor_copy(
+                x_codes[:, c * HALF : (c + 1) * HALF], x_table[:].indirect(offs_t[:, c * HALF // 16 : (c + 1) * HALF // 16])
+            )
+        w1_low = sbuf([P, H // 2], U8, "w1_low", "x_table")
+        deal_bytes(w1_low, w1_plane, 0, 2)
         deal_words(w2_codes, w2_raw)
         deal_bytes(w2_dealt, w2_plane)
 
-        def first_product(tag, codes, plane, t):
-            bank = psum.tile([P, S], F32, name=tag, tag=tag)
+        def first_product(dst, codes, plane, t, a, b):
             nc.tensor.matmul_mx(
-                out=bank[:],
+                out=dst,
                 lhsT=codes[:, 2 * P * t : 2 * P * (t + 1)].bitcast(FP4X4),
-                lhsT_scale=plane[:, P * t : P * (t + 1)],
-                rhs=x_codes[:].bitcast(FP8X4),
-                rhs_scale=x_picked[:],
+                lhsT_scale=plane,
+                rhs=x_codes[:, a:b].bitcast(FP8X4),
+                rhs_scale=x_picked[:, a:b],
                 start=True,
                 stop=True,
             )
-            return bank
 
-        y = [first_product("bank%d" % t, w1_codes, w1_dealt, t) for t in range(PACK)]
-        us = [first_product("bank%d" % (PACK + t), w2_codes, w2_dealt, t) for t in range(PACK)]
+        def bank(i, name):
+            return psum.tile([P, S], F32, name=name, tag="bank%d" % i)
 
-        window = [keep.tile([P, 2 * S], F32, name="window%d" % t) for t in range(PACK)]
-        sig = [keep.tile([P, S], F32, name="sig%d" % t) for t in range(PACK)]
-        lns = [keep.tile([P, S], F32, name="lns%d" % t) for t in range(PACK)]
-        nsp = [keep.tile([P, S], F32, name="nsp%d" % t) for t in range(PACK)]
-        pp = [keep.tile([P, S], F32, name="pp%d" % t) for t in range(PACK)]
-        low = [keep.tile([P, S], F32, name="low%d" % t) for t in range(PACK)]
-        over = [keep.tile([P, S], F32, name="over%d" % t) for t in range(PACK)]
-        cut = [keep.tile([P, S], F32, name="cut%d" % t) for t in range(PACK)]
-        held = [keep.tile([P, S], F32, name="held%d" % t) for t in range(PACK)]
-        span = [keep.tile([P, 2, S], F32, name="span%d" % h) for h in range(2)]
-        hid = [keep.tile([P, PACK, b - a], BF16, name="hid%d" % i) for i, (a, b) in enumerate(PIECES)]
-
+        y_half = [bank(c, "y_half%d" % c) for c in range(2)]
+        for c in range(2):
+            for u in range(2):
+                first_product(y_half[c][:, u * HALF : (u + 1) * HALF], w1_codes, w1_high[:, P * u : P * (u + 1)], 2 + u, c * HALF, (c + 1) * HALF)
+        y = [bank(2 + t, "y%d" % t) for t in range(2)]
+        for t in range(2):
+            first_product(y[t][:], w1_codes, w1_low[:, P * t : P * (t + 1)], t, 0, S)
+        us = [bank(PACK + t, "us%d" % t) for t in range(PACK)]
         for t in range(PACK):
-            nc.scalar.activation(sig[t][:], y[t][:], ACT.Sigmoid, scale=-1.0)
-        for t in range(PACK):
+            first_product(us[t][:], w2_codes, w2_dealt[:, P * t : P * (t + 1)], t, 0, S)
+
+        window = [sbuf([P, 2 * S], F32, "window%d" % t) for t in range(PACK)]
+        sig = [sbuf([P, 2, S], F32, "sig%d" % h) for h in range(2)]
+        lns = [sbuf([P, 2, S], F32, "lns%d" % h) for h in range(2)]
+        nsp = [sbuf([P, 2, S], F32, "nsp%d" % h) for h in range(2)]
+        pp = [sbuf([P, S], F32, "pp%d" % t) for t in range(PACK)]
+        low = {}
+        over = {t: sbuf([P, S], F32, "over%d" % t) for t in range(TURNED, PACK)}
+        cut = {t: sbuf([P, S], F32, "cut%d" % t) for t in range(TURNED, PACK)}
+        held = {t: sbuf([P, S], F32, "held%d" % t) for t in range(TURNED, PACK)}
+        span = {t: sbuf([P, S], F32, "span%d" % t) for t in range(TURNED, PACK)}
+        neg_dn = [sbuf([P, S], F32, "neg_dn%d" % t) for t in range(TURNED)]
+        pow_turned = [sbuf([P, S], F32, "pow_turned%d" % t) for t in range(TURNED)]
+        capped = [sbuf([P, S], F32, "capped%d" % t) for t in range(TURNED)]
+        held_turned = [sbuf([P, S], F32, "held_turned%d" % t) for t in range(TURNED)]
+        hid = sbuf([P, PACK, S], BF16, "hid")
+
+        y_parts = [(y[t][:], lambda pair, t=t: pair[0][:, t, :]) for t in range(2)]
+        y_parts.extend(
+            (y_half[c][:].rearrange("p (u j) -> p u j", u=2), lambda pair, c=c: pair[1][:, :, c * HALF : (c + 1) * HALF])
+            for c in range(2)
+        )
+
+        def gate(t):
             nc.scalar.activation(window[t][:, S:], us[t][:], ACT.Sigmoid, scale=2.0)
-        for h in range(2):
-            nc.vector.tensor_tensor(span[h][:], rup_t[h][:], rdn_t[h][:], ALU.add)
-        for t in range(PACK):
-            nc.scalar.activation(lns[t][:], sig[t][:], ACT.Ln, bias=TINY)
 
-        def softplus(t):
-            nc.vector.scalar_tensor_tensor(nsp[t][:], y[t][:], -1.0, lns[t][:], ALU.mult, ALU.min)
+        def ramp(tiles, t):
+            return tiles[t // 2][:, t % 2, :]
+
+        def turn(dst, src, opens=True, closes=True):
+            for c in range(S // P):
+                cols = slice(c * P, (c + 1) * P)
+                nc.tensor.matmul(
+                    dst[:, cols],
+                    src[:, cols],
+                    ident[:],
+                    start=opens and (closes or c == 0),
+                    stop=closes and (opens or c == S // P - 1),
+                    is_transpose=True,
+                )
+
+        def softplus(i):
+            src, view = y_parts[i]
+            nc.vector.scalar_tensor_tensor(view(nsp), src, -1.0, view(lns), ALU.mult, ALU.min)
 
         def power(t):
-            nc.vector.scalar_tensor_tensor(window[t][:, :S], nsp[t][:], -0.5, window[t][:, S:], ALU.add, ALU.mult)
+            h, u = divmod(t, 2)
+            nc.vector.scalar_tensor_tensor(window[t][:, :S], nsp[h][:, u, :], -0.5, window[t][:, S:], ALU.add, ALU.mult)
+
+        def look_up(t):
             nc.scalar.activation(pp[t][:], window[t][:].indirect(prv_t[:]), ACT.Copy, scale=-0.6)
 
-        softplus(0)
+        for src, view in y_parts[2:] + y_parts[:2]:
+            nc.scalar.activation(view(sig), src, ACT.Sigmoid, scale=-1.0)
         for t in range(PACK):
-            if t + 1 < PACK:
-                softplus(t + 1)
-            power(t)
+            gate(t)
+        for src, view in y_parts:
+            nc.scalar.activation(view(lns), view(sig), ACT.Ln, bias=TINY)
+        for t in range(TURNED):
+            nc.vector.tensor_scalar(neg_dn[t][:], ramp(rdn_t, t), -1.0, None, ALU.mult)
+        for t in range(TURNED, PACK):
+            nc.vector.tensor_tensor(span[t][:], ramp(rup_t, t), ramp(rdn_t, t), ALU.add)
+
+        ceil, floor, back = {}, {}, {}
+
+        def open_bounds(t, ceil_bank, floor_bank):
+            ceil[t] = bank(ceil_bank, "ceil%d" % t)
+            turn(ceil[t], ramp(rup_t, t), closes=False)
+            floor[t] = bank(floor_bank, "floor%d" % t)
+            turn(floor[t], neg_dn[t], closes=False)
+
+        def turn_power(t, pow_bank):
+            turned = bank(pow_bank, "pow_bank%d" % t)
+            turn(turned, window[t])
+            look_up(t)
+            nc.scalar.activation(pow_turned[t][:], turned[:], ACT.Copy, scale=-0.6)
+
+        def close_bounds(t):
+            turn(ceil[t], pp[t], opens=False)
+            turn(floor[t], pp[t], opens=False)
+
+        def cap(t):
+            nc.vector.tensor_tensor(capped[t][:], pow_turned[t][:], ceil[t][:], ALU.min)
+
+        def hold(t, back_bank):
+            nc.vector.tensor_tensor(held_turned[t][:], capped[t][:], floor[t][:], ALU.max)
+            back[t] = bank(back_bank, "back%d" % t)
+            turn(back[t], held_turned[t])
 
         def ramp_steps(t, a, b):
-            h, u = divmod(t, 2)
-            dn = rdn_t[h][:, u, a:b]
-            steps = [
-                lambda: nc.vector.tensor_tensor(low[t][:, a:b], pp[t][:, a:b], dn, ALU.subtract),
+            return [
+                lambda: nc.vector.tensor_tensor(low[t][:, a:b], pp[t][:, a:b], ramp(rdn_t, t)[:, a:b], ALU.subtract),
                 lambda: nc.vector.scalar_tensor_tensor(
                     over[t][:, a:b], window[t][:, a:b], -0.6, low[t][:, a:b], ALU.mult, ALU.subtract
                 ),
-                lambda: nc.vector.tensor_tensor(cut[t][:, a:b], over[t][:, a:b], span[h][:, u, a:b], ALU.min),
+                lambda: nc.vector.tensor_tensor(cut[t][:, a:b], over[t][:, a:b], span[t][:, a:b], ALU.min),
                 lambda: nc.vector.scalar_tensor_tensor(
                     held[t][:, a:b], cut[t][:, a:b], 0.0, low[t][:, a:b], ALU.max, ALU.add
                 ),
             ]
-            return steps
 
-        def hidden(t, i):
-            a, b = PIECES[i]
+        def hidden(t, a, b):
+            src = back[t] if t < TURNED else held[t]
             nc.vector.scalar_tensor_tensor(
-                hid[i][:, t, :], held[t][:, a:b], unit_t[:, t : t + 1], window[t][:, S + a : S + b], ALU.mult, ALU.mult
+                hid[:, t, a:b], src[:, a:b], unit_t[:, t : t + 1], window[t][:, S + a : S + b], ALU.mult, ALU.mult
             )
 
         out_v = out.rearrange("(a p) j -> p a j", p=P)
+        woven = [sbuf([P, b - a, PACK], BF16, "woven%d" % i) for i, (a, b) in enumerate(PIECES)]
 
-        def last_product(i, engine_copy):
+        def weave(i, copy):
+            a, b = PIECES[i]
+            copy(out=woven[i][:], in_=hid[:, :, a:b].rearrange("p t j -> p j t"))
+
+        def last_product(i, copy, queue):
             a, b = PIECES[i]
             n = b - a
-            woven = keep.tile([P, n, PACK], BF16, name="woven%d" % i, align_bytes=64)
-            codes = keep.tile([P, n], U32, name="hcodes%d" % i, align_bytes=64)
-            plane = keep.tile([P, n], U8, name="hplane%d" % i, align_bytes=64)
-            engine_copy(out=woven[:], in_=hid[i][:].rearrange("p t j -> p j t"))
+            codes = sbuf([P, n], U32, "hcodes%d" % i)
+            plane = sbuf([P, n], U8, "hplane%d" % i)
             nc.vector.quantize_mx(
-                out=codes[:].bitcast(FP8X4), scales=plane[:], in_=woven[:].rearrange("p j t -> p (j t)")
+                out=codes[:].bitcast(FP8X4), scales=plane[:], in_=woven[i][:].rearrange("p j t -> p (j t)")
             )
-            tag = "bank%d" % (PACK + i)
-            bank = psum.tile([P, S], F32, name="zones%d" % i, tag=tag)
+            zones = bank((5, 7, 0)[i], "zones%d" % i)
             for m in range(N // P):
                 nc.tensor.matmul_mx(
-                    out=bank[:, m * n : (m + 1) * n],
+                    out=zones[:, m * n : (m + 1) * n],
                     lhsT=w3_codes[:, 2 * P * m : 2 * P * (m + 1)].bitcast(FP4X4),
                     lhsT_scale=w3_plane[:, P * m : P * (m + 1)],
                     rhs=codes[:].bitcast(FP8X4),
@@ -202,21 +276,53 @@ def tile_picked_yunitc_ramp_p_kernel(
                     start=True,
                     stop=True,
                 )
-            res = keep.tile([P, N // P, n], F32, name="res%d" % i)
-            nc.scalar.copy(out=res[:].rearrange("p a j -> p (a j)"), in_=bank[:, : (N // P) * n])
-            nc.sync.dma_start(out=out_v[:, :, a:b], in_=res[:])
+            res = sbuf([P, N // P, n], F32, "res%d" % i)
+            copy(out=res[:].rearrange("p a j -> p (a j)"), in_=zones[:, : (N // P) * n])
+            queue.dma_start(out=out_v[:, :, a:b], in_=res[:])
 
-        for s0, s1 in zip(ramp_steps(0, 0, S), ramp_steps(1, 0, S)):
-            s0()
-            s1()
-        for i in range(len(PIECES)):
-            hidden(0, i)
-            hidden(1, i)
-        for i, (a, b) in enumerate(PIECES):
-            for s0, s1 in zip(ramp_steps(2, a, b), ramp_steps(3, a, b)):
-                s0()
-                s1()
-            hidden(2, i)
-            hidden(3, i)
-            last = i == len(PIECES) - 1
-            last_product(i, nc.vector.tensor_copy if last else nc.scalar.copy)
+        open_bounds(0, 4, 5)
+        open_bounds(1, 6, 7)
+        softplus(0)
+        softplus(1)
+        for t in range(TURNED):
+            power(t)
+            turn_power(t, 2 + t)
+        for t in range(TURNED):
+            close_bounds(t)
+        softplus(2)
+        softplus(3)
+        for t in range(TURNED, PACK):
+            power(t)
+            look_up(t)
+        third, early, late = ramp_steps(2, 0, S), ramp_steps(3, 0, HALF), ramp_steps(3, HALF, S)
+        cap(0)
+        hold(0, 4)
+        cap(1)
+        low[2] = sbuf([P, S], F32, "low2", "pow_turned1")
+        third[0]()
+        hold(1, 6)
+        low[3] = sbuf([P, S], F32, "low3", "capped1")
+        third[1]()
+        hidden(0, 0, S)
+        third[2]()
+        early[0]()
+        third[3]()
+        early[1]()
+        hidden(1, 0, HALF)
+        early[2]()
+        hidden(2, 0, HALF)
+        early[3]()
+        late[0]()
+        hidden(3, 0, HALF)
+        weave(0, nc.scalar.copy)
+        late[1]()
+        hidden(1, HALF, S)
+        late[2]()
+        hidden(2, HALF, S)
+        late[3]()
+        last_product(0, nc.scalar.copy, nc.sync)
+        for i in (1, 2):
+            hidden(3, *PIECES[i])
+            weave(i, nc.scalar.copy if i == 1 else nc.vector.tensor_copy)
+        last_product(1, nc.scalar.copy, nc.scalar)
+        last_product(2, nc.vector.tensor_copy, nc.sync)

from contextlib import ExitStack

import concourse.mybir as mybir
from concourse.masks import make_identity

K, T, S, N, H = 512, 2048, 512, 256, 512
FLOPS = 2 * (2 * K * H * S + H * N * S)

P = 128
PACK = 4
QUADS = 4
HALF = S // 2
F32 = mybir.dt.float32
BF16 = mybir.dt.bfloat16
I32 = mybir.dt.int32
U32 = mybir.dt.uint32
U16 = mybir.dt.uint16
U8 = mybir.dt.uint8
FP8X4 = mybir.dt.float8_e4m3fn_x4
FP4X4 = mybir.dt.float4_e2m1fn_x4
ALU = mybir.AluOpType
ACT = mybir.ActivationFunctionType

TINY = 2.0 ** -60
TURNED = 2
PIECES = ((0, 256), (256, 384), (384, 512))


def load_scale_rows(queue, plane, scales, quads=range(QUADS)):
    for q in quads:
        queue.dma_start(
            out=plane[32 * q : 32 * q + 4, :].bitcast(I32),
            in_=scales[0, 4 * q : 4 * q + 4, :].bitcast(I32),
        )


def tile_picked_yunitc_ramp_p_kernel(
    tc, x_words, x_scales, w1_words, w1_scales, w2_words, w2_scales, rup, rdn, unit, w3_words, w3_scales, offs, prv, out
):
    nc = tc.nc
    with ExitStack() as ctx:
        lists = ctx.enter_context(tc.tile_pool(name="lists", bufs=1))
        keep = ctx.enter_context(tc.tile_pool(name="keep", bufs=1))
        psum = ctx.enter_context(tc.psum_pool(name="psum", bufs=1))

        def sbuf(shape, dtype, name, slot=None):
            return keep.tile(shape, dtype, name=name, tag=slot or name, align_bytes=64)

        offs_t = lists.tile([P, S // 16], U16, name="offs_t")
        prv_t = lists.tile([P, S // 16], U16, name="prv_t")

        x_plane = sbuf([P, T], U8, "x_plane")
        w1_plane = sbuf([P, H], U8, "w1_plane")
        w2_plane = sbuf([P, H], U8, "w2_plane")
        w3_plane = sbuf([P, N], U8, "w3_plane")
        nc.vector.memset(x_plane[:, : T // 2].bitcast(I32), 0)
        nc.gpsimd.memset(x_plane[:, T // 2 :].bitcast(I32), 0)
        for plane in (w1_plane, w2_plane, w3_plane):
            nc.gpsimd.memset(plane[:].bitcast(I32), 0)

        x_table = sbuf([P, T], U32, "x_table")
        w1_raw = sbuf([P, 2 * H], U8, "w1_raw")
        w2_raw = sbuf([P, 2 * H], U8, "w2_raw")
        w3_codes = sbuf([P, 2 * N], U8, "w3_codes")
        unit_t = sbuf([P, PACK], F32, "unit_t")
        rdn_t = [sbuf([P, 2, S], F32, "rdn%d" % h) for h in range(2)]
        rup_t = [sbuf([P, 2, S], F32, "rup%d" % h) for h in range(2)]

        nc.sync.dma_start(offs_t[:], offs)
        nc.scalar.dma_start(out=w1_raw[:].bitcast(I32), in_=w1_words[0].bitcast(I32))
        load_scale_rows(nc.sync, x_plane, x_scales, (0, 2))
        load_scale_rows(nc.scalar, x_plane, x_scales, (1, 3))
        nc.sync.dma_start(out=x_table[:].bitcast(I32), in_=x_words[0].rearrange("p c r -> p (c r)").bitcast(I32))
        load_scale_rows(nc.scalar, w1_plane, w1_scales)
        load_scale_rows(nc.sync, w2_plane, w2_scales, (0, 1))
        nc.sync.dma_start(out=w2_raw[:].bitcast(I32), in_=w2_words[0].bitcast(I32))
        load_scale_rows(nc.gpsimd, w2_plane, w2_scales, (2, 3))
        rup_v = rup.rearrange("(p t) j -> p t j", t=PACK)
        rdn_v = rdn.rearrange("(p t) j -> p t j", t=PACK)
        for h in range(2):
            nc.sync.dma_start(out=rdn_t[h][:], in_=rdn_v[:, 2 * h : 2 * h + 2, :])
            nc.sync.dma_start(out=rup_t[h][:], in_=rup_v[:, 2 * h : 2 * h + 2, :])
        nc.sync.dma_start(prv_t[:], prv)
        nc.sync.dma_start(out=unit_t[:], in_=unit.rearrange("(p t) o -> p (t o)", t=PACK))
        nc.sync.dma_start(out=w3_codes[:].bitcast(I32), in_=w3_words[0].bitcast(I32))
        load_scale_rows(nc.sync, w3_plane, w3_scales)

        ident = sbuf([P, P], F32, "ident")
        make_identity(nc, ident[:])

        w1_codes = sbuf([P, 2 * H], U8, "w1_codes")
        w2_codes = sbuf([P, 2 * H], U8, "w2_codes")
        w1_high = sbuf([P, H // 2], U8, "w1_high")
        w2_dealt = sbuf([P, H], U8, "w2_dealt")
        x_codes = sbuf([P, S], U32, "x_codes")
        x_picked = sbuf([P, S], U8, "x_picked")

        def deal_words(dst, src):
            nc.vector.tensor_copy(
                out=dst[:].rearrange("p (t m b) -> p t m b", t=PACK, b=2),
                in_=src[:].rearrange("p (m t b) -> p t m b", t=PACK, b=2),
            )

        def deal_bytes(dst, src, t0=0, t1=PACK):
            nc.vector.tensor_copy(
                out=dst[:].rearrange("p (t m) -> p t m", m=P),
                in_=src[:].rearrange("p (m t) -> p t m", t=PACK)[:, t0:t1, :],
            )

        deal_words(w1_codes, w1_raw)
        nc.vector.tensor_copy(x_picked[:], x_plane[:].indirect(offs_t[:]))
        deal_bytes(w1_high, w1_plane, 2, 4)
        for c in range(2):
            nc.vector.tensor_copy(
                x_codes[:, c * HALF : (c + 1) * HALF], x_table[:].indirect(offs_t[:, c * HALF // 16 : (c + 1) * HALF // 16])
            )
        w1_low = sbuf([P, H // 2], U8, "w1_low", "x_table")
        deal_bytes(w1_low, w1_plane, 0, 2)
        deal_words(w2_codes, w2_raw)
        deal_bytes(w2_dealt, w2_plane)

        def first_product(dst, codes, plane, t, a, b):
            nc.tensor.matmul_mx(
                out=dst,
                lhsT=codes[:, 2 * P * t : 2 * P * (t + 1)].bitcast(FP4X4),
                lhsT_scale=plane,
                rhs=x_codes[:, a:b].bitcast(FP8X4),
                rhs_scale=x_picked[:, a:b],
                start=True,
                stop=True,
            )

        def bank(i, name):
            return psum.tile([P, S], F32, name=name, tag="bank%d" % i)

        y_half = [bank(c, "y_half%d" % c) for c in range(2)]
        for c in range(2):
            for u in range(2):
                first_product(y_half[c][:, u * HALF : (u + 1) * HALF], w1_codes, w1_high[:, P * u : P * (u + 1)], 2 + u, c * HALF, (c + 1) * HALF)
        y = [bank(2 + t, "y%d" % t) for t in range(2)]
        for t in range(2):
            first_product(y[t][:], w1_codes, w1_low[:, P * t : P * (t + 1)], t, 0, S)
        us = [bank(PACK + t, "us%d" % t) for t in range(PACK)]
        for t in range(PACK):
            first_product(us[t][:], w2_codes, w2_dealt[:, P * t : P * (t + 1)], t, 0, S)

        window = [sbuf([P, 2 * S], F32, "window%d" % t) for t in range(PACK)]
        sig = [sbuf([P, 2, S], F32, "sig%d" % h) for h in range(2)]
        lns = [sbuf([P, 2, S], F32, "lns%d" % h) for h in range(2)]
        nsp = [sbuf([P, 2, S], F32, "nsp%d" % h) for h in range(2)]
        pp = [sbuf([P, S], F32, "pp%d" % t) for t in range(PACK)]
        low = {}
        over = {t: sbuf([P, S], F32, "over%d" % t) for t in range(TURNED, PACK)}
        cut = {t: sbuf([P, S], F32, "cut%d" % t) for t in range(TURNED, PACK)}
        held = {t: sbuf([P, S], F32, "held%d" % t) for t in range(TURNED, PACK)}
        span = {t: sbuf([P, S], F32, "span%d" % t) for t in range(TURNED, PACK)}
        neg_dn = [sbuf([P, S], F32, "neg_dn%d" % t) for t in range(TURNED)]
        pow_turned = [sbuf([P, S], F32, "pow_turned%d" % t) for t in range(TURNED)]
        capped = [sbuf([P, S], F32, "capped%d" % t) for t in range(TURNED)]
        held_turned = [sbuf([P, S], F32, "held_turned%d" % t) for t in range(TURNED)]
        hid = sbuf([P, PACK, S], BF16, "hid")

        y_parts = [(y[t][:], lambda pair, t=t: pair[0][:, t, :]) for t in range(2)]
        y_parts.extend(
            (y_half[c][:].rearrange("p (u j) -> p u j", u=2), lambda pair, c=c: pair[1][:, :, c * HALF : (c + 1) * HALF])
            for c in range(2)
        )

        def gate(t):
            nc.scalar.activation(window[t][:, S:], us[t][:], ACT.Sigmoid, scale=2.0)

        def ramp(tiles, t):
            return tiles[t // 2][:, t % 2, :]

        def turn(dst, src, opens=True, closes=True):
            for c in range(S // P):
                cols = slice(c * P, (c + 1) * P)
                nc.tensor.matmul(
                    dst[:, cols],
                    src[:, cols],
                    ident[:],
                    start=opens and (closes or c == 0),
                    stop=closes and (opens or c == S // P - 1),
                    is_transpose=True,
                )

        def softplus(i):
            src, view = y_parts[i]
            nc.vector.scalar_tensor_tensor(view(nsp), src, -1.0, view(lns), ALU.mult, ALU.min)

        def power(t):
            h, u = divmod(t, 2)
            nc.vector.scalar_tensor_tensor(window[t][:, :S], nsp[h][:, u, :], -0.5, window[t][:, S:], ALU.add, ALU.mult)

        def look_up(t):
            nc.scalar.activation(pp[t][:], window[t][:].indirect(prv_t[:]), ACT.Copy, scale=-0.6)

        for src, view in y_parts[2:] + y_parts[:2]:
            nc.scalar.activation(view(sig), src, ACT.Sigmoid, scale=-1.0)
        for t in range(PACK):
            gate(t)
        for src, view in y_parts:
            nc.scalar.activation(view(lns), view(sig), ACT.Ln, bias=TINY)
        for t in range(TURNED):
            nc.vector.tensor_scalar(neg_dn[t][:], ramp(rdn_t, t), -1.0, None, ALU.mult)
        for t in range(TURNED, PACK):
            nc.vector.tensor_tensor(span[t][:], ramp(rup_t, t), ramp(rdn_t, t), ALU.add)

        ceil, floor, back = {}, {}, {}

        def open_bounds(t, ceil_bank, floor_bank):
            ceil[t] = bank(ceil_bank, "ceil%d" % t)
            turn(ceil[t], ramp(rup_t, t), closes=False)
            floor[t] = bank(floor_bank, "floor%d" % t)
            turn(floor[t], neg_dn[t], closes=False)

        def turn_power(t, pow_bank):
            turned = bank(pow_bank, "pow_bank%d" % t)
            turn(turned, window[t])
            look_up(t)
            nc.scalar.activation(pow_turned[t][:], turned[:], ACT.Copy, scale=-0.6)

        def close_bounds(t):
            turn(ceil[t], pp[t], opens=False)
            turn(floor[t], pp[t], opens=False)

        def cap(t):
            nc.vector.tensor_tensor(capped[t][:], pow_turned[t][:], ceil[t][:], ALU.min)

        def hold(t, back_bank):
            nc.vector.tensor_tensor(held_turned[t][:], capped[t][:], floor[t][:], ALU.max)
            back[t] = bank(back_bank, "back%d" % t)
            turn(back[t], held_turned[t])

        def ramp_steps(t, a, b):
            return [
                lambda: nc.vector.tensor_tensor(low[t][:, a:b], pp[t][:, a:b], ramp(rdn_t, t)[:, a:b], ALU.subtract),
                lambda: nc.vector.scalar_tensor_tensor(
                    over[t][:, a:b], window[t][:, a:b], -0.6, low[t][:, a:b], ALU.mult, ALU.subtract
                ),
                lambda: nc.vector.tensor_tensor(cut[t][:, a:b], over[t][:, a:b], span[t][:, a:b], ALU.min),
                lambda: nc.vector.scalar_tensor_tensor(
                    held[t][:, a:b], cut[t][:, a:b], 0.0, low[t][:, a:b], ALU.max, ALU.add
                ),
            ]

        def hidden(t, a, b):
            src = back[t] if t < TURNED else held[t]
            nc.vector.scalar_tensor_tensor(
                hid[:, t, a:b], src[:, a:b], unit_t[:, t : t + 1], window[t][:, S + a : S + b], ALU.mult, ALU.mult
            )

        out_v = out.rearrange("(a p) j -> p a j", p=P)
        woven = [sbuf([P, b - a, PACK], BF16, "woven%d" % i) for i, (a, b) in enumerate(PIECES)]

        def weave(i, copy):
            a, b = PIECES[i]
            copy(out=woven[i][:], in_=hid[:, :, a:b].rearrange("p t j -> p j t"))

        def last_product(i, copy, queue):
            a, b = PIECES[i]
            n = b - a
            codes = sbuf([P, n], U32, "hcodes%d" % i)
            plane = sbuf([P, n], U8, "hplane%d" % i)
            nc.vector.quantize_mx(
                out=codes[:].bitcast(FP8X4), scales=plane[:], in_=woven[i][:].rearrange("p j t -> p (j t)")
            )
            zones = bank((5, 7, 0)[i], "zones%d" % i)
            for m in range(N // P):
                nc.tensor.matmul_mx(
                    out=zones[:, m * n : (m + 1) * n],
                    lhsT=w3_codes[:, 2 * P * m : 2 * P * (m + 1)].bitcast(FP4X4),
                    lhsT_scale=w3_plane[:, P * m : P * (m + 1)],
                    rhs=codes[:].bitcast(FP8X4),
                    rhs_scale=plane[:],
                    start=True,
                    stop=True,
                )
            res = sbuf([P, N // P, n], F32, "res%d" % i)
            copy(out=res[:].rearrange("p a j -> p (a j)"), in_=zones[:, : (N // P) * n])
            queue.dma_start(out=out_v[:, :, a:b], in_=res[:])

        open_bounds(0, 4, 5)
        open_bounds(1, 6, 7)
        softplus(0)
        softplus(1)
        for t in range(TURNED):
            power(t)
            turn_power(t, 2 + t)
        for t in range(TURNED):
            close_bounds(t)
        softplus(2)
        softplus(3)
        for t in range(TURNED, PACK):
            power(t)
            look_up(t)
        third, early, late = ramp_steps(2, 0, S), ramp_steps(3, 0, HALF), ramp_steps(3, HALF, S)
        cap(0)
        hold(0, 4)
        cap(1)
        low[2] = sbuf([P, S], F32, "low2", "pow_turned1")
        third[0]()
        hold(1, 6)
        low[3] = sbuf([P, S], F32, "low3", "capped1")
        third[1]()
        hidden(0, 0, S)
        third[2]()
        early[0]()
        third[3]()
        early[1]()
        hidden(1, 0, HALF)
        early[2]()
        hidden(2, 0, HALF)
        early[3]()
        late[0]()
        hidden(3, 0, HALF)
        weave(0, nc.scalar.copy)
        late[1]()
        hidden(1, HALF, S)
        late[2]()
        hidden(2, HALF, S)
        late[3]()
        last_product(0, nc.scalar.copy, nc.sync)
        for i in (1, 2):
            hidden(3, *PIECES[i])
            weave(i, nc.scalar.copy if i == 1 else nc.vector.tensor_copy)
        last_product(1, nc.scalar.copy, nc.scalar)
        last_product(2, nc.vector.tensor_copy, nc.sync)
